import numpy as np
CORES = [5,6,7,13,14,15]
N = 6
ROOT = 4
def setup_inputs(rng):
    return {"x": rng.standard_normal((N, 128, N * 4), dtype=np.float32)}
def reference(x):
    return {"y": np.stack([x[ROOT][:, r * 4:(r + 1) * 4] for r in range(N)])}

from concourse.bass import DstId, RemoteDMATransfer

BLOCK = 4

SCRATCH = {
    "stage": ("sbuf", [128, 24], "float32"),
    "land": ("sbuf", [128, BLOCK], "float32"),
}
SEMAPHORES = ["loaded", "sent", "arrived", "stored"]


def engine_masks(T, topo):
    root_core = T.cores[T.root]
    masks = {}
    off, on = 0, 8
    for dst in T.cores:
        if dst == root_core:
            continue
        if topo.chip(dst) != topo.chip(root_core):
            masks[dst] = (0x3 << off, 2)
            off += 2
        else:
            masks[dst] = (0xF << on, 4)
            on += 4
    return masks


def rank_program(g, core, T, topo):
    rank = T.rank_of(core)
    if rank is None:
        return
    masks = engine_masks(T, topo)

    if rank == T.root:
        g.sync.dma_start(T.stage[:], T.x[:]).then_inc(T.sem.loaded, 16)
        g.scalar.dma_start(T.y[:], T.x[:, rank * BLOCK:(rank + 1) * BLOCK]).then_inc(T.sem.stored, 16)
        g.wait_ge(T.sem.loaded, 16)
        transfers = []
        total = 0
        for r, dst in enumerate(T.cores):
            if dst == core:
                continue
            rid, pid, _se = topo.addr(dst)
            mask, n = masks[dst]
            total += n
            transfers.append(RemoteDMATransfer(
                dst_ids=[DstId(rid=rid, pnc=pid)],
                dma_engine_mask=mask,
                remote_sem=T.sem.arrived,
                src=T.stage[:, r * BLOCK:(r + 1) * BLOCK],
                dst=T.land[:],
            ))
        g.remote_dma_fused(transfers, local_sem=T.sem.sent)
        g.wait_ge(T.sem.sent, total)
        g.wait_ge(T.sem.stored, 16)
    else:
        g.sync.wait_ge(T.sem.arrived, masks[core][1])
        g.sync.dma_start(T.y[:], T.land[:]).then_inc(T.sem.stored, 16)
        g.sync.wait_ge(T.sem.stored, 16)
